import numpy as np
import ml_dtypes

BF16 = ml_dtypes.bfloat16


def bf(x):
    return np.asarray(x, np.float32).astype(BF16)


def f32(x):
    return np.asarray(x, np.float32)


def f64(x):
    return np.asarray(x).astype(np.float64)


def striped(idx):
    return np.concatenate([l.reshape(-1, 16).T for l in idx])


def rows(idx, k):
    return np.tile(np.repeat(idx, 16, axis=0), (k // (16 * 8), 1))


def look(tab, idx):
    return np.take_along_axis(f64(tab), rows(idx, len(tab)), axis=1)


K, S, V, N = 128, 2048, 1536, 1536


def setup_inputs():
    return {"tab": f32(np.random.standard_normal((2, K, S))), "y": f32(np.random.standard_normal((K, V))), "offs": striped(np.stack([np.random.permutation(S)[:N] for _ in range(8)]))}


def reference(tab, y, offs):
    idx = np.stack([g.T.reshape(-1) for g in np.split(offs, 8)])
    x = (np.maximum(look(tab[0], idx), f64(y))) * (np.maximum(look(tab[1], idx), 0.0))
    return x

@@ -1,0 +1,43 @@
+import concourse.mybir as mybir
+
+F32 = mybir.dt.float32
+U16 = mybir.dt.uint16
+MAX = mybir.AluOpType.max
+MULT = mybir.AluOpType.mult
+RELU = mybir.ActivationFunctionType.Relu
+
+P = 128
+S = 2048
+N = 1536
+PIECE = 512
+LANES = 16
+
+
+def tile_lookup_vg_maxrelu_out_kernel(tc, tab, y, offs, out):
+    nc = tc.nc
+    with (
+        tc.tile_pool(name="held", bufs=1) as held,
+        tc.tile_pool(name="pieces", bufs=N // PIECE) as pieces,
+    ):
+        offsets = held.tile([P, N // LANES], U16)
+        values = held.tile([P, S], F32)
+        gates = held.tile([P, S], F32)
+        stream = held.tile([P, N], F32)
+        nc.sync.dma_start(offsets[:], offs)
+        nc.sync.dma_start(values[:], tab[0])
+        nc.sync.dma_start(stream[:], y)
+        nc.sync.dma_start(gates[:], tab[1])
+
+        for first in range(0, N, PIECE):
+            cols = slice(first, first + PIECE)
+            listed = offsets[:, first // LANES : (first + PIECE) // LANES]
+
+            larger = pieces.tile([P, PIECE], F32)
+            nc.vector.tensor_tensor(larger[:], values[:].indirect(listed), stream[:, cols], MAX)
+
+            gate = pieces.tile([P, PIECE], F32)
+            nc.scalar.activation(gate[:], gates[:].indirect(listed), RELU)
+
+            product = pieces.tile([P, PIECE], F32)
+            nc.vector.tensor_tensor(product[:], larger[:], gate[:], MULT)
+            nc.sync.dma_start(out[:, cols], product[:])

@@ -23,6 +23,11 @@ def tile_lookup_vg_maxrelu_out_kernel(tc, tab, y, offs, out):
         values = held.tile([P, S], F32)
         gates = held.tile([P, S], F32)
         stream = held.tile([P, N], F32)
+        zeros = held.tile([P, 1], F32)
+        warmed = held.tile([P, 1], F32)
+        nc.vector.memset(zeros[:], 0.0)
+        nc.scalar.activation(warmed[:], zeros[:], RELU)
+
         nc.sync.dma_start(offsets[:], offs)
         nc.sync.dma_start(values[:], tab[0])
         nc.sync.dma_start(stream[:], y)

@@ -15,34 +15,35 @@ LANES = 16
 
 def tile_lookup_vg_maxrelu_out_kernel(tc, tab, y, offs, out):
     nc = tc.nc
+    starts = range(0, N, PIECE)
     with (
         tc.tile_pool(name="held", bufs=1) as held,
-        tc.tile_pool(name="pieces", bufs=N // PIECE) as pieces,
+        tc.tile_pool(name="pieces", bufs=len(starts)) as pieces,
     ):
-        offsets = held.tile([P, N // LANES], U16)
-        values = held.tile([P, S], F32)
-        gates = held.tile([P, S], F32)
-        stream = held.tile([P, N], F32)
         zeros = held.tile([P, 1], F32)
         warmed = held.tile([P, 1], F32)
         nc.vector.memset(zeros[:], 0.0)
         nc.scalar.activation(warmed[:], zeros[:], RELU)
 
+        offsets = held.tile([P, N // LANES], U16)
+        values = held.tile([P, S], F32)
+        gates = held.tile([P, S], F32)
+        streams = [pieces.tile([P, PIECE], F32, name="stream") for start in starts]
         nc.sync.dma_start(offsets[:], offs)
         nc.sync.dma_start(values[:], tab[0])
-        nc.sync.dma_start(stream[:], y)
+        nc.sync.dma_start(streams[0][:], y[:, :PIECE])
         nc.sync.dma_start(gates[:], tab[1])
+        for stream, start in zip(streams[1:], starts[1:]):
+            nc.sync.dma_start(stream[:], y[:, start : start + PIECE])
 
-        for first in range(0, N, PIECE):
-            cols = slice(first, first + PIECE)
-            listed = offsets[:, first // LANES : (first + PIECE) // LANES]
+        larger = [pieces.tile([P, PIECE], F32, name="larger") for start in starts]
+        gate = [pieces.tile([P, PIECE], F32, name="gate") for start in starts]
+        for i, start in enumerate(starts):
+            listed = offsets[:, start // LANES : (start + PIECE) // LANES]
+            nc.vector.tensor_tensor(larger[i][:], values[:].indirect(listed), streams[i][:], MAX)
+            nc.scalar.activation(gate[i][:], gates[:].indirect(listed), RELU)
 
-            larger = pieces.tile([P, PIECE], F32)
-            nc.vector.tensor_tensor(larger[:], values[:].indirect(listed), stream[:, cols], MAX)
-
-            gate = pieces.tile([P, PIECE], F32)
-            nc.scalar.activation(gate[:], gates[:].indirect(listed), RELU)
-
+        for i, start in enumerate(starts):
             product = pieces.tile([P, PIECE], F32)
-            nc.vector.tensor_tensor(product[:], larger[:], gate[:], MULT)
-            nc.sync.dma_start(out[:, cols], product[:])
+            nc.vector.tensor_tensor(product[:], larger[i][:], gate[i][:], MULT)
+            nc.sync.dma_start(out[:, start : start + PIECE], product[:])

@@ -28,19 +28,21 @@ def tile_lookup_vg_maxrelu_out_kernel(tc, tab, y, offs, out):
         offsets = held.tile([P, N // LANES], U16)
         values = held.tile([P, S], F32)
         gates = held.tile([P, S], F32)
-        streams = [pieces.tile([P, PIECE], F32, name="stream") for start in starts]
+        early = 2 * PIECE
+        stream_early = held.tile([P, early], F32)
+        stream_late = held.tile([P, N - early], F32)
+        streams = [stream_early[:, :PIECE], stream_early[:, PIECE:], stream_late[:]]
         nc.sync.dma_start(offsets[:], offs)
         nc.sync.dma_start(values[:], tab[0])
-        nc.sync.dma_start(streams[0][:], y[:, :PIECE])
+        nc.sync.dma_start(stream_early[:], y[:, :early])
         nc.sync.dma_start(gates[:], tab[1])
-        for stream, start in zip(streams[1:], starts[1:]):
-            nc.sync.dma_start(stream[:], y[:, start : start + PIECE])
+        nc.sync.dma_start(stream_late[:], y[:, early:])
 
         larger = [pieces.tile([P, PIECE], F32, name="larger") for start in starts]
         gate = [pieces.tile([P, PIECE], F32, name="gate") for start in starts]
         for i, start in enumerate(starts):
             listed = offsets[:, start // LANES : (start + PIECE) // LANES]
-            nc.vector.tensor_tensor(larger[i][:], values[:].indirect(listed), streams[i][:], MAX)
+            nc.vector.tensor_tensor(larger[i][:], values[:].indirect(listed), streams[i], MAX)
             nc.scalar.activation(gate[i][:], gates[:].indirect(listed), RELU)
 
         for i, start in enumerate(starts):

import concourse.mybir as mybir

F32 = mybir.dt.float32
U16 = mybir.dt.uint16
MAX = mybir.AluOpType.max
MULT = mybir.AluOpType.mult
RELU = mybir.ActivationFunctionType.Relu

P = 128
S = 2048
N = 1536
PIECE = 512
LANES = 16


def tile_lookup_vg_maxrelu_out_kernel(tc, tab, y, offs, out):
    nc = tc.nc
    starts = range(0, N, PIECE)
    with (
        tc.tile_pool(name="held", bufs=1) as held,
        tc.tile_pool(name="pieces", bufs=len(starts)) as pieces,
    ):
        zeros = held.tile([P, 1], F32)
        warmed = held.tile([P, 1], F32)
        nc.vector.memset(zeros[:], 0.0)
        nc.scalar.activation(warmed[:], zeros[:], RELU)

        offsets = held.tile([P, N // LANES], U16)
        values = held.tile([P, S], F32)
        gates = held.tile([P, S], F32)
        early = 2 * PIECE
        stream_early = held.tile([P, early], F32)
        stream_late = held.tile([P, N - early], F32)
        streams = [stream_early[:, :PIECE], stream_early[:, PIECE:], stream_late[:]]
        nc.sync.dma_start(offsets[:], offs)
        nc.sync.dma_start(values[:], tab[0])
        nc.sync.dma_start(stream_early[:], y[:, :early])
        nc.sync.dma_start(gates[:], tab[1])
        nc.sync.dma_start(stream_late[:], y[:, early:])

        larger = [pieces.tile([P, PIECE], F32, name="larger") for start in starts]
        gate = [pieces.tile([P, PIECE], F32, name="gate") for start in starts]
        for i, start in enumerate(starts):
            listed = offsets[:, start // LANES : (start + PIECE) // LANES]
            nc.vector.tensor_tensor(larger[i][:], values[:].indirect(listed), streams[i], MAX)
            nc.scalar.activation(gate[i][:], gates[:].indirect(listed), RELU)

        for i, start in enumerate(starts):
            product = pieces.tile([P, PIECE], F32)
            nc.vector.tensor_tensor(product[:], larger[i][:], gate[i][:], MULT)
            nc.sync.dma_start(out[:, start : start + PIECE], product[:])
